import numpy as np
import ml_dtypes


def mxq(x, axis, fmt="e4m3"):
    dtype, down = {"e4m3": (ml_dtypes.float8_e4m3fn, 7), "e5m2": (ml_dtypes.float8_e5m2, 14)}[fmt]
    v = np.moveaxis(np.asarray(x, np.float32).astype(ml_dtypes.bfloat16).astype(np.float64), axis, -1)
    blocks = v.reshape(v.shape[:-1] + (-1, 32))
    amax = np.abs(blocks).max(-1, keepdims=True)
    byte = np.maximum(np.where(amax > 0, np.frexp(amax)[1] - 1 + 127, 0) - down, 1)
    scale = np.exp2(byte - 127.0)
    codes = (blocks / scale).astype(np.float32).astype(dtype).astype(np.float64)
    return np.moveaxis((codes * scale).reshape(v.shape), -1, axis)


WIDE = False


def mx_kscale(k):
    if not WIDE:
        return np.ones(k)
    levels = np.array([10, -10, 5, -5, 0])
    if k % 512:
        return np.exp2(np.random.permutation(np.resize(levels, k // 32))).repeat(32)
    a = np.empty((k // 512, 16))
    for p in range(k // 512):
        a[p, :8] = np.random.permutation(np.resize(levels, 8))
        for g in range(8):
            far = levels[np.abs(levels - a[p, g]) >= 10]
            a[p, g + 8] = far[np.random.randint(len(far))]
    return np.exp2(a.ravel()).repeat(32)


BF16 = ml_dtypes.bfloat16


def bf(x):
    return np.asarray(x, np.float32).astype(BF16)


def f64(x):
    return np.asarray(x).astype(np.float64)


E2M1 = np.array([0.0, 0.5, 1.0, 1.5, 2.0, 3.0, 4.0, 6.0, -0.0, -0.5, -1.0, -1.5, -2.0, -3.0, -4.0, -6.0])


def pack_weight(w, fmt):
    k, n = w.shape
    w = f64(bf(w)).reshape(k // 32, 32, n)
    amax = np.abs(w).max(1)
    if fmt == "e4m3":
        byte = np.frexp(amax)[1] - 1 + 127 - 7
    else:
        mant, ex = np.frexp(amax / 6.0)
        byte = np.where(mant > 0.5, ex, ex - 1) + 127
    byte = np.clip(np.where(amax > 0, byte, 1), 1, 254)
    scaled = (w * np.exp2(127.0 - byte)[:, None, :]).reshape(k, n).astype(np.float32)
    by_word = np.ascontiguousarray(scaled.reshape(k // 512, 128, 4, n).transpose(0, 1, 3, 2))
    if fmt == "e4m3":
        words = by_word.astype(ml_dtypes.float8_e4m3fn).view(np.uint8)
    else:
        c = by_word.astype(ml_dtypes.float4_e2m1fn).view(np.uint8) & 0xF
        words = c[..., 0::2] | (c[..., 1::2] << 4)
    return np.ascontiguousarray(words), np.ascontiguousarray(byte.astype(np.uint8).reshape(k // 512, 16, n))


def unpack_weight(words, scales, fmt):
    g, p, n, _ = words.shape
    if fmt == "e4m3":
        vals = np.ascontiguousarray(words).view(ml_dtypes.float8_e4m3fn).astype(np.float64)
    else:
        nib = np.empty((g, p, n, 4), np.uint8)
        nib[..., 0::2] = words & 0xF
        nib[..., 1::2] = words >> 4
        vals = E2M1[nib]
    vals = vals * np.repeat(np.exp2(scales.astype(np.float64) - 127.0), 8, axis=1)[..., None]
    return vals.transpose(0, 1, 3, 2).reshape(g * 512, n)
def pack4(w):
    words, scales = pack_weight(w, "e2m1")
    return words.reshape(words.shape[0], 128, -1), scales


def unpack4(words, scales):
    return unpack_weight(words.reshape(words.shape[0], 128, -1, 2), scales, "e2m1")


M, K, F, D, R = 2048, 1024, 1024, 1024, 512


def setup_inputs():
    s = mx_kscale(K)
    d = mx_kscale(D)
    t = mx_kscale(F)
    obs = np.random.standard_normal((M, K)) * s
    w = np.random.standard_normal((K, F)) / np.sqrt(K) / s[:, None]
    target = np.random.standard_normal((M, F))
    gain = (1 + 0.1 * np.random.standard_normal(F)) / np.sqrt(F) * t
    code_words, code_scales = pack4(np.random.standard_normal((D, F)) * d[:, None] / t)
    skill_words, skill_scales = pack4(np.random.standard_normal((D, R)) / np.sqrt(D) / d[:, None])
    return {"obs": bf(obs), "w": bf(w), "target": bf(target), "gain": bf(gain),
            "code_words": code_words, "code_scales": code_scales,
            "skill_words": skill_words, "skill_scales": skill_scales}


def reference(obs, w, target, gain, code_words, code_scales, skill_words, skill_scales):
    pred = mxq(f64(obs), 1, "e4m3") @ mxq(f64(w), 0, "e4m3")
    err = pred - f64(target)
    novelty = f64(gain) * np.square(err)
    codes = unpack4(code_words, code_scales)
    skills = unpack4(skill_words, skill_scales)
    v = codes.T @ skills
    bonus = mxq(novelty, 1, "e4m3") @ mxq(v, 0, "e4m3")
    return bonus

@@ -1,0 +1,376 @@
+from contextlib import ExitStack
+
+import concourse.mybir as mybir
+from concourse.masks import make_identity
+
+M, K, F, D, R = 2048, 1024, 1024, 1024, 512
+FLOPS = 2 * M * K * F + 2 * D * F * R + 2 * M * F * R
+
+F32 = mybir.dt.float32
+BF16 = mybir.dt.bfloat16
+I32 = mybir.dt.int32
+U32 = mybir.dt.uint32
+U8 = mybir.dt.uint8
+FP8X4 = mybir.dt.float8_e4m3fn_x4
+FP4X4 = mybir.dt.float4_e2m1fn_x4
+ALU = mybir.AluOpType
+ACT = mybir.ActivationFunctionType
+
+P = 128
+PACK = 4
+KP = P * PACK
+NG = 2
+NT = M // P
+
+
+def tile_skill_novelty_bonus_s12_kernel(
+    tc, obs, w, target, gain, code_words, code_scales, skill_words, skill_scales, out
+):
+    nc = tc.nc
+    with ExitStack() as ctx:
+        keep = ctx.enter_context(tc.tile_pool(name="keep", bufs=1))
+        work = ctx.enter_context(tc.tile_pool(name="work", bufs=2))
+        psum = ctx.enter_context(tc.psum_pool(name="psum", bufs=8))
+        ctx.enter_context(tc.manual_schedule())
+
+        def bank(name):
+            return psum.tile([P, KP], F32, name=name, tag="bank")
+
+        ident = keep.tile([P, P], F32, name="ident")
+        make_identity(nc, ident[:])
+        a_scale_raw = keep.tile([P, NG, F], U8, name="a_scale_raw", align_bytes=64)
+        b_scale = keep.tile([P, NG, R], U8, name="b_scale", align_bytes=64)
+        gain_rows32 = keep.tile([P, P], F32, name="gain_rows32")
+        half = keep.tile([P, NG * PACK], F32, name="half")
+        nc.gpsimd.memset(gain_rows32[:], 0.0)
+        nc.gpsimd.memset(half[:], 0.5)
+        nc.vector.memset(a_scale_raw[:].rearrange("p g n -> p (g n)").bitcast(I32), 0)
+        nc.vector.memset(b_scale[:].rearrange("p g n -> p (g n)").bitcast(I32), 0)
+        warm = keep.tile([P, 1], F32, name="warm")
+        nc.scalar.activation(out=warm[:], in_=half[:, 0:1], func=ACT.Square)
+
+        obs_sb, tgt_sb, w_raw = {}, {}, {}
+
+        def load_obs(tiles):
+            n = len(tiles)
+            t = keep.tile([P, n, K], BF16, name="obs%d" % tiles[0], align_bytes=64)
+            rows = obs[tiles[0] * P : (tiles[0] + n) * P, :]
+            nc.sync.dma_start(out=t[:], in_=rows.rearrange("(i p) k -> p i k", p=P))
+            for j, i in enumerate(tiles):
+                obs_sb[i] = t[:, j, :]
+
+        def load_target(tiles, gs):
+            n = len(tiles)
+            width = KP * len(gs)
+            t = keep.tile([P, n, width], BF16, name="tgt%d_%d" % (tiles[0], gs[0]), align_bytes=64)
+            rows = target[tiles[0] * P : (tiles[0] + n) * P, gs[0] * KP : gs[0] * KP + width]
+            nc.sync.dma_start(out=t[:], in_=rows.rearrange("(i p) k -> p i k", p=P))
+            for j, i in enumerate(tiles):
+                for jg, g in enumerate(gs):
+                    tgt_sb[i, g] = t[:, j, jg * KP : (jg + 1) * KP]
+
+        def load_w(kg, g):
+            t = keep.tile([P, PACK, KP], BF16, name="w%d%d" % (kg, g), align_bytes=64)
+            rows = w[kg * KP : (kg + 1) * KP, g * KP : (g + 1) * KP]
+            nc.sync.dma_start(out=t[:], in_=rows.rearrange("(p j) n -> p j n", j=PACK))
+            w_raw[kg, g] = t
+
+        gain_rows = keep.tile([NG * PACK, P], BF16, name="gain_rows")
+        a_raw = keep.tile([P, NG, 2 * F], U8, name="a_raw", align_bytes=64)
+        b_words = keep.tile([P, NG, 2 * R], U8, name="b_words", align_bytes=64)
+
+        def load_codes():
+            nc.sync.dma_start(out=a_raw[:].bitcast(I32), in_=code_words.rearrange("g p n -> p g n").bitcast(I32))
+            nc.sync.dma_start(out=b_words[:].bitcast(I32), in_=skill_words.rearrange("g p n -> p g n").bitcast(I32))
+            for plane, rows in ((a_scale_raw, code_scales), (b_scale, skill_scales)):
+                for q in range(4):
+                    nc.sync.dma_start(
+                        out=plane[32 * q : 32 * q + 4, :, :].bitcast(I32),
+                        in_=rows[:, 4 * q : 4 * q + 4, :].rearrange("g r n -> r g n").bitcast(I32),
+                    )
+
+        units = [((0, 1, 2, 3), (0,)), ((0, 1, 2, 3), (1,))]
+        units += [((i, i + 1), (0, 1)) for i in range(4, NT - 2, 2)]
+        units += [((NT - 2,), (0, 1)), ((NT - 1,), (0, 1))]
+
+        load_w(0, 0)
+        load_obs((0,))
+        load_w(1, 0)
+        load_obs((1,))
+        load_obs((2, 3))
+        load_target(*units[0])
+        load_w(0, 1)
+        load_w(1, 1)
+        for g in range(NG):
+            nc.sync.dma_start(
+                out=gain_rows[g * PACK : (g + 1) * PACK, :].rearrange("t (q r) -> t q r", r=8),
+                in_=gain[g * KP : (g + 1) * KP].rearrange("(q t r) -> t q r", t=PACK, r=8),
+            )
+        load_obs((4, 5))
+        load_target(*units[1])
+        load_codes()
+        for i in range(6, NT, 2):
+            load_obs((i, i + 1))
+            load_target((i - 2, i - 1), (0, 1))
+        load_target((NT - 2, NT - 1), (0, 1))
+
+        def interleave(engine, dst, src):
+            d = dst.rearrange("p (c i) t -> p c t i", i=4)
+            s = src.rearrange("p t (c i) -> p c t i", i=4)
+            if engine == "v":
+                nc.vector.tensor_copy(out=d, in_=s)
+            else:
+                nc.scalar.copy(out=d, in_=s)
+
+        def grouped_tile(name):
+            return work.tile([P, KP, PACK], BF16, name=name, tag="grouped", bufs=3, align_bytes=64)
+
+        def quantize(codes, scales, grouped):
+            nc.vector.quantize_mx(out=codes.bitcast(FP8X4), scales=scales, in_=grouped)
+
+        w_grouped, w_codes, w_scales = {}, {}, {}
+
+        def w_interleave(kg, g, vec_cols):
+            t = grouped_tile("wg%d%d" % (kg, g))
+            if vec_cols:
+                interleave("v", t[:, :vec_cols, :], w_raw[kg, g][:, :, :vec_cols])
+            if vec_cols < KP:
+                interleave("s", t[:, vec_cols:, :], w_raw[kg, g][:, :, vec_cols:])
+            w_grouped[kg, g] = t
+
+        def w_quantize(kg, g):
+            w_codes[kg, g] = keep.tile([P, KP], U32, name="wc%d%d" % (kg, g), align_bytes=64)
+            w_scales[kg, g] = keep.tile([P, KP], U8, name="ws%d%d" % (kg, g), align_bytes=64)
+            quantize(w_codes[kg, g][:], w_scales[kg, g][:], w_grouped[kg, g][:].rearrange("p c t -> p (c t)"))
+
+        obs_grouped, obs_codes, obs_scales = {}, {}, {}
+
+        def obs_transpose(i):
+            words = obs_sb[i].bitcast(F32)
+            b = bank("obsT%d" % i)
+            for kg in range(NG):
+                for u in range(2):
+                    j = 2 * kg + u
+                    nc.tensor.transpose(
+                        b[:, j * P : (j + 1) * P], words[:, 256 * kg + u : 256 * (kg + 1) : 2], ident[:]
+                    )
+            t = work.tile([P, NG, P, 2], F32, name="og%d" % i, tag="og", bufs=4, align_bytes=64)
+            nc.scalar.copy(out=t[:], in_=b[:].rearrange("p (g u m) -> p g m u", g=NG, u=2))
+            obs_grouped[i] = t
+
+        def obs_quantize(i):
+            obs_codes[i] = work.tile([P, NG * P], U32, name="oc%d" % i, tag="oc", bufs=8, align_bytes=64)
+            obs_scales[i] = work.tile([P, NG * P], U8, name="os%d" % i, tag="os", bufs=8, align_bytes=64)
+            quantize(
+                obs_codes[i][:],
+                obs_scales[i][:],
+                obs_grouped[i][:].rearrange("p g m u -> p (g m u)").bitcast(BF16),
+            )
+
+        err = {}
+
+        def predict(i, g):
+            b = bank("pred%d_%d" % (i, g))
+            for kg in range(NG):
+                cols = slice(kg * P, (kg + 1) * P)
+                nc.tensor.matmul_mx(
+                    out=b[:],
+                    lhsT=obs_codes[i][:, cols].bitcast(FP8X4),
+                    lhsT_scale=obs_scales[i][:, cols],
+                    rhs=w_codes[kg, g][:].bitcast(FP8X4),
+                    rhs_scale=w_scales[kg, g][:],
+                    start=(kg == 0),
+                    stop=(kg == NG - 1),
+                )
+            e = work.tile([P, KP], F32, name="err%d_%d" % (i, g), tag="err", bufs=6, align_bytes=64)
+            nc.vector.tensor_tensor(
+                out=e[:].rearrange("p (t q r) -> p t q r", t=PACK, r=8),
+                in0=b[:].rearrange("p (q t r) -> p t q r", t=PACK, r=8),
+                in1=tgt_sb[i, g].rearrange("p (q t r) -> p t q r", t=PACK, r=8),
+                op=ALU.subtract,
+            )
+            err[i, g] = e
+
+        gain_root = keep.tile([P, NG * PACK], F32, name="gain_root")
+        gain_sign = keep.tile([P, NG * PACK], F32, name="gain_sign")
+
+        def gain_setup_transpose():
+            nc.vector.tensor_copy(out=gain_rows32[0 : NG * PACK, :], in_=gain_rows[:])
+            b = bank("gainT")
+            nc.tensor.transpose(b[:, 0:P], gain_rows32[:], ident[:])
+            twice = keep.tile([P, NG * PACK], F32, name="twice")
+            mag = keep.tile([P, NG * PACK], F32, name="mag")
+            nc.vector.tensor_scalar(twice[:], b[:, 0 : NG * PACK], 0.0, 2.0, ALU.is_ge, ALU.mult)
+            nc.vector.tensor_scalar(gain_sign[:], twice[:], -1.0, None, ALU.add)
+            nc.vector.tensor_tensor(out=mag[:], in0=b[:, 0 : NG * PACK], in1=gain_sign[:], op=ALU.mult)
+            nc.gpsimd.tensor_tensor(out=gain_root[:], in0=mag[:], in1=half[:], op=ALU.pow)
+
+        squares, nov_grouped, nov_codes, nov_scales = {}, {}, {}, {}
+
+        def err_transpose(tiles, g):
+            n = len(tiles)
+            width = n * P
+            sq = work.tile([P, PACK, width], BF16, name="sq%d_%d" % (tiles[0], g), tag="sq", bufs=4, align_bytes=64)
+            per_bank = PACK // n
+            for t0 in range(0, PACK, per_bank):
+                b = bank("errT%d_%d_%d" % (tiles[0], g, t0))
+                for s in range(per_bank):
+                    for j, i in enumerate(tiles):
+                        c0 = s * width + j * P
+                        t = t0 + s
+                        nc.tensor.transpose(b[:, c0 : c0 + P], err[i, g][:, t * P : (t + 1) * P], ident[:])
+                for s in range(per_bank):
+                    t = t0 + s
+                    nc.scalar.activation(
+                        out=sq[:, t, :],
+                        in_=b[:, s * width : (s + 1) * width],
+                        func=ACT.Square,
+                        scale=gain_root[:, g * PACK + t : g * PACK + t + 1],
+                    )
+            squares[tiles, g] = sq
+
+        def nov_interleave(tiles, g):
+            t = grouped_tile("ng%d_%d" % (tiles[0], g))
+            width = len(tiles) * P
+            interleave("v", t[:, :width, :], squares[tiles, g][:])
+            nov_grouped[tiles, g] = t
+
+        def nov_quantize(tiles, g):
+            width = len(tiles) * P
+            c = work.tile([P, width], U32, name="nc%d_%d" % (tiles[0], g), tag="nc", bufs=6, align_bytes=64)
+            s = work.tile([P, width], U8, name="ns%d_%d" % (tiles[0], g), tag="ns", bufs=6, align_bytes=64)
+            quantize(c[:], s[:], nov_grouped[tiles, g][:, :width, :].rearrange("p c t -> p (c t)"))
+            for j, i in enumerate(tiles):
+                nov_codes[i, g] = c[:, j * P : (j + 1) * P]
+                nov_scales[i, g] = s[:, j * P : (j + 1) * P]
+
+        a_words = keep.tile([P, NG, 2 * F], U8, name="a_words", align_bytes=64)
+        a_scale = keep.tile([P, NG, F], U8, name="a_scale", align_bytes=64)
+
+        def a_permute():
+            for dst, src, run in ((a_words, a_raw, 4), (a_scale, a_scale_raw, 2)):
+                d = dst[:].rearrange("p g n -> p (g n)").bitcast(I32)
+                s = src[:].rearrange("p g n -> p (g n)").bitcast(I32)
+                nc.vector.tensor_copy(
+                    out=d.rearrange("p (h t q r) -> p h t q r", t=PACK, q=16, r=run),
+                    in_=s.rearrange("p (h q t r) -> p h t q r", t=PACK, q=16, r=run),
+                )
+
+        v_rows, v_grouped, v_codes, v_scales = {}, {}, {}, {}
+
+        def v_matmul(g, t):
+            if t == 0:
+                v_rows[g] = work.tile([P, PACK, R], BF16, name="vr%d" % g, tag="sq", bufs=4, align_bytes=64)
+            b = bank("v%d_%d" % (g, t))
+            c0 = g * KP + t * P
+            for dg in range(NG):
+                nc.tensor.matmul_mx(
+                    out=b[:],
+                    lhsT=a_words[:, dg, 2 * c0 : 2 * (c0 + P)].bitcast(FP4X4),
+                    lhsT_scale=a_scale[:, dg, c0 : c0 + P],
+                    rhs=b_words[:, dg, :].bitcast(FP4X4),
+                    rhs_scale=b_scale[:, dg, :],
+                    start=(dg == 0),
+                    stop=(dg == NG - 1),
+                )
+            nc.scalar.activation(
+                out=v_rows[g][:, t, :],
+                in_=b[:],
+                func=ACT.Copy,
+                scale=gain_sign[:, g * PACK + t : g * PACK + t + 1],
+            )
+
+        def v_interleave(g):
+            v_grouped[g] = grouped_tile("vg%d" % g)
+            interleave("v", v_grouped[g][:], v_rows[g][:])
+
+        def v_quantize(g):
+            v_codes[g] = keep.tile([P, R], U32, name="vc%d" % g, align_bytes=64)
+            v_scales[g] = keep.tile([P, R], U8, name="vs%d" % g, align_bytes=64)
+            quantize(v_codes[g][:], v_scales[g][:], v_grouped[g][:].rearrange("p c t -> p (c t)"))
+
+        def bonus(i):
+            b = bank("bonus%d" % i)
+            for g in range(NG):
+                nc.tensor.matmul_mx(
+                    out=b[:],
+                    lhsT=nov_codes[i, g].bitcast(FP8X4),
+                    lhsT_scale=nov_scales[i, g],
+                    rhs=v_codes[g][:].bitcast(FP8X4),
+                    rhs_scale=v_scales[g][:],
+                    start=(g == 0),
+                    stop=(g == NG - 1),
+                )
+            res = work.tile([P, R], F32, name="res%d" % i, tag="res", bufs=4)
+            nc.scalar.copy(out=res[:], in_=b[:])
+            nc.sync.dma_start(out=out[i * P : (i + 1) * P, :], in_=res[:])
+
+        w_interleave(0, 0, KP)
+        obs_transpose(0)
+        w_quantize(0, 0)
+        obs_quantize(0)
+        w_interleave(1, 0, KP // 2)
+        obs_transpose(1)
+        w_quantize(1, 0)
+        obs_quantize(1)
+        obs_transpose(2)
+        obs_transpose(3)
+        obs_quantize(2)
+        obs_quantize(3)
+
+        n_units = len(units)
+        obs_next = 4
+        ready = []
+        for step in range(n_units + 1):
+            halves = []
+            if step < n_units:
+                tiles, gs = units[step]
+                halves = [(i, g) for g in gs for i in tiles]
+            if step in (1, 2):
+                extra = [lambda g=step - 1, t=t: v_matmul(g, t) for t in range(PACK)]
+            elif step > 2:
+                take = ready[:2] if step < n_units - 3 else ready[:3]
+                ready = ready[len(take) :]
+                extra = [lambda i=i: bonus(i) for i in take]
+            else:
+                extra = []
+            if step == 0:
+                w_interleave(0, 1, 0)
+            n_pairs = (len(halves) + 1) // 2
+            per = (len(extra) + max(n_pairs, 1) - 1) // max(n_pairs, 1)
+            for j in range(max(n_pairs, 1)):
+                for i, g in halves[2 * j : 2 * j + 2]:
+                    predict(i, g)
+                for job in extra[j * per : (j + 1) * per]:
+                    job()
+            if step == 0:
+                gain_setup_transpose()
+                w_quantize(0, 1)
+                w_interleave(1, 1, KP // 2)
+                a_permute()
+                w_quantize(1, 1)
+            prev = []
+            if step >= 1:
+                ptiles, pgs = units[step - 1]
+                prev = [(ptiles, g) for g in pgs]
+            new_obs = [i for i in range(obs_next, min(obs_next + 2, NT))]
+            obs_next += len(new_obs)
+            for pt, g in prev:
+                nov_interleave(pt, g)
+            if step in (1, 2):
+                v_interleave(step - 1)
+            for i in new_obs:
+                obs_transpose(i)
+            for pt, g in prev:
+                nov_quantize(pt, g)
+            if step in (1, 2):
+                v_quantize(step - 1)
+            for i in new_obs:
+                obs_quantize(i)
+            if prev and prev[-1][1] == NG - 1:
+                ready = ready + list(prev[-1][0])
+            if step < n_units:
+                for g in gs:
+                    err_transpose(tiles, g)
+        for i in ready:
+            bonus(i)

@@ -21,6 +21,30 @@ PACK = 4
 KP = P * PACK
 NG = 2
 NT = M // P
+V_HEAD = 5
+B_FIRST = 7
+W10_V = 512
+W01_V = 256
+W11_V = 256
+VIL0 = 1
+VIL1 = 4
+TAILV = 2
+PRESORT = 8
+VIL0_S = 256
+VIL1_S = 256
+B_LAST = 18
+V_COPY = 4
+W00_V = 256
+T0 = 4
+LEAD = 5
+V2 = 1
+SORT_S = 8
+HEAD_SORT = 0
+EARLYQ = 1
+SINGLE = 1
+RV0 = 10
+RV1 = 16
+RVP = 1
 
 
 def tile_skill_novelty_bonus_s12_kernel(
@@ -40,12 +64,12 @@ def tile_skill_novelty_bonus_s12_kernel(
         make_identity(nc, ident[:])
         a_scale_raw = keep.tile([P, NG, F], U8, name="a_scale_raw", align_bytes=64)
         b_scale = keep.tile([P, NG, R], U8, name="b_scale", align_bytes=64)
-        gain_rows32 = keep.tile([P, P], F32, name="gain_rows32")
+        gain_rows32 = keep.tile([P, NG * P], F32, name="gain_rows32")
         half = keep.tile([P, NG * PACK], F32, name="half")
-        nc.gpsimd.memset(gain_rows32[:], 0.0)
         nc.gpsimd.memset(half[:], 0.5)
         nc.vector.memset(a_scale_raw[:].rearrange("p g n -> p (g n)").bitcast(I32), 0)
         nc.vector.memset(b_scale[:].rearrange("p g n -> p (g n)").bitcast(I32), 0)
+        nc.vector.memset(gain_rows32[:], 0.0)
         warm = keep.tile([P, 1], F32, name="warm")
         nc.scalar.activation(out=warm[:], in_=half[:, 0:1], func=ACT.Square)
 
@@ -75,40 +99,39 @@ def tile_skill_novelty_bonus_s12_kernel(
             nc.sync.dma_start(out=t[:], in_=rows.rearrange("(p j) n -> p j n", j=PACK))
             w_raw[kg, g] = t
 
-        gain_rows = keep.tile([NG * PACK, P], BF16, name="gain_rows")
+        gain_rows = keep.tile([PACK, NG * P], BF16, name="gain_rows")
         a_raw = keep.tile([P, NG, 2 * F], U8, name="a_raw", align_bytes=64)
         b_words = keep.tile([P, NG, 2 * R], U8, name="b_words", align_bytes=64)
 
-        def load_codes():
-            nc.sync.dma_start(out=a_raw[:].bitcast(I32), in_=code_words.rearrange("g p n -> p g n").bitcast(I32))
-            nc.sync.dma_start(out=b_words[:].bitcast(I32), in_=skill_words.rearrange("g p n -> p g n").bitcast(I32))
-            for plane, rows in ((a_scale_raw, code_scales), (b_scale, skill_scales)):
-                for q in range(4):
-                    nc.sync.dma_start(
-                        out=plane[32 * q : 32 * q + 4, :, :].bitcast(I32),
-                        in_=rows[:, 4 * q : 4 * q + 4, :].rearrange("g r n -> r g n").bitcast(I32),
-                    )
+        def load_scales(queue, plane, rows):
+            for q in range(4):
+                queue.dma_start(
+                    out=plane[32 * q : 32 * q + 4, :, :].bitcast(I32),
+                    in_=rows[:, 4 * q : 4 * q + 4, :].rearrange("g r n -> r g n").bitcast(I32),
+                )
 
-        units = [((0, 1, 2, 3), (0,)), ((0, 1, 2, 3), (1,))]
-        units += [((i, i + 1), (0, 1)) for i in range(4, NT - 2, 2)]
-        units += [((NT - 2,), (0, 1)), ((NT - 1,), (0, 1))]
+        units = [((0, 1), 0), ((2, 3), 0), ((0, 1), 1), ((2, 3), 1)]
+        units += [((i, i + 1), g) for i in range(4, NT, 2) for g in range(NG)]
+        units = units[:-SINGLE] + [((i,), g) for tiles, g in units[-SINGLE:] for i in tiles]
 
+        nc.sync.dma_start(
+            out=gain_rows[:].rearrange("t (q r) -> t q r", r=8),
+            in_=gain.rearrange("(q t r) -> t q r", t=PACK, r=8),
+        )
+        load_scales(nc.sync, a_scale_raw, code_scales)
+        load_obs((0, 1))
+        nc.sync.dma_start(out=a_raw[:].bitcast(I32), in_=code_words.rearrange("g p n -> p g n").bitcast(I32))
+        nc.sync.dma_start(out=b_words[:].bitcast(I32), in_=skill_words.rearrange("g p n -> p g n").bitcast(I32))
+        load_scales(nc.sync, b_scale, skill_scales)
         load_w(0, 0)
-        load_obs((0,))
         load_w(1, 0)
-        load_obs((1,))
         load_obs((2, 3))
-        load_target(*units[0])
+        load_target((0, 1), (0,))
         load_w(0, 1)
+        load_target((2, 3), (0,))
         load_w(1, 1)
-        for g in range(NG):
-            nc.sync.dma_start(
-                out=gain_rows[g * PACK : (g + 1) * PACK, :].rearrange("t (q r) -> t q r", r=8),
-                in_=gain[g * KP : (g + 1) * KP].rearrange("(q t r) -> t q r", t=PACK, r=8),
-            )
         load_obs((4, 5))
-        load_target(*units[1])
-        load_codes()
+        load_target((0, 1, 2, 3), (1,))
         for i in range(6, NT, 2):
             load_obs((i, i + 1))
             load_target((i - 2, i - 1), (0, 1))
@@ -123,7 +146,7 @@ def tile_skill_novelty_bonus_s12_kernel(
                 nc.scalar.copy(out=d, in_=s)
 
         def grouped_tile(name):
-            return work.tile([P, KP, PACK], BF16, name=name, tag="grouped", bufs=3, align_bytes=64)
+            return work.tile([P, KP, PACK], BF16, name=name, tag="grouped", bufs=4, align_bytes=64)
 
         def quantize(codes, scales, grouped):
             nc.vector.quantize_mx(out=codes.bitcast(FP8X4), scales=scales, in_=grouped)
@@ -145,15 +168,28 @@ def tile_skill_novelty_bonus_s12_kernel(
 
         obs_grouped, obs_codes, obs_scales = {}, {}, {}
 
+        obs_sorted = {}
+
+        def obs_sort(i):
+            t = work.tile([P, NG, 2, P], F32, name="osort%d" % i, tag="osort", bufs=3, align_bytes=64)
+            words = obs_sb[i].bitcast(F32)
+            if i < SORT_S:
+                nc.vector.tensor_copy(out=t[:], in_=words.rearrange("p (g j u) -> p g u j", g=NG, u=2))
+            else:
+                nc.scalar.copy(out=t[:], in_=words.rearrange("p (g j u) -> p g u j", g=NG, u=2))
+            obs_sorted[i] = t
+
         def obs_transpose(i):
             words = obs_sb[i].bitcast(F32)
             b = bank("obsT%d" % i)
             for kg in range(NG):
                 for u in range(2):
                     j = 2 * kg + u
-                    nc.tensor.transpose(
-                        b[:, j * P : (j + 1) * P], words[:, 256 * kg + u : 256 * (kg + 1) : 2], ident[:]
-                    )
+                    if i in obs_sorted:
+                        src = obs_sorted[i][:, kg, u, :]
+                    else:
+                        src = words[:, 256 * kg + u : 256 * (kg + 1) : 2]
+                    nc.tensor.transpose(b[:, j * P : (j + 1) * P], src, ident[:])
             t = work.tile([P, NG, P, 2], F32, name="og%d" % i, tag="og", bufs=4, align_bytes=64)
             nc.scalar.copy(out=t[:], in_=b[:].rearrange("p (g u m) -> p g m u", g=NG, u=2))
             obs_grouped[i] = t
@@ -195,14 +231,21 @@ def tile_skill_novelty_bonus_s12_kernel(
         gain_sign = keep.tile([P, NG * PACK], F32, name="gain_sign")
 
         def gain_setup_transpose():
-            nc.vector.tensor_copy(out=gain_rows32[0 : NG * PACK, :], in_=gain_rows[:])
+            nc.vector.tensor_copy(out=gain_rows32[0:PACK, :], in_=gain_rows[:])
             b = bank("gainT")
-            nc.tensor.transpose(b[:, 0:P], gain_rows32[:], ident[:])
+            for g in range(NG):
+                nc.tensor.transpose(b[:, g * P : (g + 1) * P], gain_rows32[:, g * P : (g + 1) * P], ident[:])
+            by_part = b[:, : NG * P].rearrange("p (g c) -> p g c", g=NG)[:, :, 0:PACK]
             twice = keep.tile([P, NG * PACK], F32, name="twice")
             mag = keep.tile([P, NG * PACK], F32, name="mag")
-            nc.vector.tensor_scalar(twice[:], b[:, 0 : NG * PACK], 0.0, 2.0, ALU.is_ge, ALU.mult)
+            nc.vector.tensor_scalar(twice[:].rearrange("p (g t) -> p g t", g=NG), by_part, 0.0, 2.0, ALU.is_ge, ALU.mult)
             nc.vector.tensor_scalar(gain_sign[:], twice[:], -1.0, None, ALU.add)
-            nc.vector.tensor_tensor(out=mag[:], in0=b[:, 0 : NG * PACK], in1=gain_sign[:], op=ALU.mult)
+            nc.vector.tensor_tensor(
+                out=mag[:].rearrange("p (g t) -> p g t", g=NG),
+                in0=by_part,
+                in1=gain_sign[:].rearrange("p (g t) -> p g t", g=NG),
+                op=ALU.mult,
+            )
             nc.gpsimd.tensor_tensor(out=gain_root[:], in0=mag[:], in1=half[:], op=ALU.pow)
 
         squares, nov_grouped, nov_codes, nov_scales = {}, {}, {}, {}
@@ -237,8 +280,8 @@ def tile_skill_novelty_bonus_s12_kernel(
 
         def nov_quantize(tiles, g):
             width = len(tiles) * P
-            c = work.tile([P, width], U32, name="nc%d_%d" % (tiles[0], g), tag="nc", bufs=6, align_bytes=64)
-            s = work.tile([P, width], U8, name="ns%d_%d" % (tiles[0], g), tag="ns", bufs=6, align_bytes=64)
+            c = work.tile([P, width], U32, name="nc%d_%d" % (tiles[0], g), tag="nc", bufs=12, align_bytes=64)
+            s = work.tile([P, width], U8, name="ns%d_%d" % (tiles[0], g), tag="ns", bufs=12, align_bytes=64)
             quantize(c[:], s[:], nov_grouped[tiles, g][:, :width, :].rearrange("p c t -> p (c t)"))
             for j, i in enumerate(tiles):
                 nov_codes[i, g] = c[:, j * P : (j + 1) * P]
@@ -256,11 +299,11 @@ def tile_skill_novelty_bonus_s12_kernel(
                     in_=s.rearrange("p (h q t r) -> p h t q r", t=PACK, q=16, r=run),
                 )
 
-        v_rows, v_grouped, v_codes, v_scales = {}, {}, {}, {}
+        v_rows, v_grouped, v_codes, v_scales, v_banks = {}, {}, {}, {}, {}
 
         def v_matmul(g, t):
             if t == 0:
-                v_rows[g] = work.tile([P, PACK, R], BF16, name="vr%d" % g, tag="sq", bufs=4, align_bytes=64)
+                v_rows[g] = work.tile([P, PACK, R], BF16, name="vr%d" % g, tag="vr", bufs=2, align_bytes=64)
             b = bank("v%d_%d" % (g, t))
             c0 = g * KP + t * P
             for dg in range(NG):
@@ -273,16 +316,22 @@ def tile_skill_novelty_bonus_s12_kernel(
                     start=(dg == 0),
                     stop=(dg == NG - 1),
                 )
+            v_banks[g, t] = b
+
+        def v_copy(g, t):
             nc.scalar.activation(
                 out=v_rows[g][:, t, :],
-                in_=b[:],
+                in_=v_banks[g, t][:],
                 func=ACT.Copy,
                 scale=gain_sign[:, g * PACK + t : g * PACK + t + 1],
             )
 
-        def v_interleave(g):
+        def v_interleave(g, s_cols):
             v_grouped[g] = grouped_tile("vg%d" % g)
-            interleave("v", v_grouped[g][:], v_rows[g][:])
+            if s_cols < R:
+                interleave("v", v_grouped[g][:, s_cols:, :], v_rows[g][:, :, s_cols:])
+            if s_cols:
+                interleave("s", v_grouped[g][:, :s_cols, :], v_rows[g][:, :, :s_cols])
 
         def v_quantize(g):
             v_codes[g] = keep.tile([P, R], U32, name="vc%d" % g, align_bytes=64)
@@ -301,76 +350,88 @@ def tile_skill_novelty_bonus_s12_kernel(
                     start=(g == 0),
                     stop=(g == NG - 1),
                 )
-            res = work.tile([P, R], F32, name="res%d" % i, tag="res", bufs=4)
-            nc.scalar.copy(out=res[:], in_=b[:])
+            res = work.tile([P, R], F32, name="res%d" % i, tag="res", bufs=6)
+            if RV0 <= i < RV1 and i % 2 == RVP:
+                nc.vector.tensor_copy(out=res[:], in_=b[:])
+            else:
+                nc.scalar.copy(out=res[:], in_=b[:])
             nc.sync.dma_start(out=out[i * P : (i + 1) * P, :], in_=res[:])
 
-        w_interleave(0, 0, KP)
+        v_jobs = [(g, t) for g in range(NG) for t in range(PACK)]
+        gain_setup_transpose()
         obs_transpose(0)
-        w_quantize(0, 0)
-        obs_quantize(0)
-        w_interleave(1, 0, KP // 2)
         obs_transpose(1)
-        w_quantize(1, 0)
+        a_permute()
+        obs_quantize(0)
         obs_quantize(1)
+        w_interleave(0, 0, W00_V)
+        for g, t in v_jobs[:T0]:
+            v_matmul(g, t)
+            v_copy(g, t)
+        w_quantize(0, 0)
+        w_interleave(1, 0, W10_V)
+        for g, t in v_jobs[T0:V_HEAD]:
+            v_matmul(g, t)
+        w_quantize(1, 0)
+        for g, t in v_jobs[T0:V_COPY]:
+            v_copy(g, t)
+        if HEAD_SORT:
+            obs_sort(2)
+            obs_sort(3)
         obs_transpose(2)
         obs_transpose(3)
-        obs_quantize(2)
-        obs_quantize(3)
+        for g, t in v_jobs[max(T0, V_COPY):V_HEAD]:
+            v_copy(g, t)
+        if EARLYQ:
+            obs_quantize(2)
+            obs_quantize(3)
+        v_jobs = v_jobs[V_HEAD:]
 
         n_units = len(units)
-        obs_next = 4
-        ready = []
-        for step in range(n_units + 1):
-            halves = []
-            if step < n_units:
-                tiles, gs = units[step]
-                halves = [(i, g) for g in gs for i in tiles]
-            if step in (1, 2):
-                extra = [lambda g=step - 1, t=t: v_matmul(g, t) for t in range(PACK)]
-            elif step > 2:
-                take = ready[:2] if step < n_units - 3 else ready[:3]
-                ready = ready[len(take) :]
-                extra = [lambda i=i: bonus(i) for i in take]
-            else:
-                extra = []
-            if step == 0:
-                w_interleave(0, 1, 0)
-            n_pairs = (len(halves) + 1) // 2
-            per = (len(extra) + max(n_pairs, 1) - 1) // max(n_pairs, 1)
-            for j in range(max(n_pairs, 1)):
-                for i, g in halves[2 * j : 2 * j + 2]:
-                    predict(i, g)
-                for job in extra[j * per : (j + 1) * per]:
-                    job()
-            if step == 0:
-                gain_setup_transpose()
+        next_bonus = 0
+        for h in range(n_units + 3):
+            live = h < n_units
+            if live:
+                tiles, g = units[h]
+                predict(tiles[0], g)
+            if 0 <= h - 3 < n_units:
+                nov_quantize(*units[h - 3])
+            if h == 0 and not EARLYQ:
+                obs_quantize(2)
+            if h >= 2 and h + 2 < NT:
+                obs_quantize(h + 2)
+            if live and len(tiles) > 1:
+                predict(tiles[1], g)
+            if h == 0 and not EARLYQ:
+                obs_quantize(3)
+            if h == 0:
+                w_interleave(0, 1, W01_V)
+            if h == 1:
                 w_quantize(0, 1)
-                w_interleave(1, 1, KP // 2)
-                a_permute()
+                w_interleave(1, 1, W11_V)
+            if v_jobs:
+                n_v = 2 if h == V2 else 1
+                for job in v_jobs[:n_v]:
+                    v_matmul(*job)
+                    v_copy(*job)
+                v_jobs = v_jobs[n_v:]
+            elif B_FIRST <= h <= B_LAST:
+                bonus(next_bonus)
+                next_bonus = next_bonus + 1
+            if h >= 1 and h + 3 < NT:
+                obs_transpose(h + 3)
+            if h == 1:
                 w_quantize(1, 1)
-            prev = []
-            if step >= 1:
-                ptiles, pgs = units[step - 1]
-                prev = [(ptiles, g) for g in pgs]
-            new_obs = [i for i in range(obs_next, min(obs_next + 2, NT))]
-            obs_next += len(new_obs)
-            for pt, g in prev:
-                nov_interleave(pt, g)
-            if step in (1, 2):
-                v_interleave(step - 1)
-            for i in new_obs:
-                obs_transpose(i)
-            for pt, g in prev:
-                nov_quantize(pt, g)
-            if step in (1, 2):
-                v_quantize(step - 1)
-            for i in new_obs:
-                obs_quantize(i)
-            if prev and prev[-1][1] == NG - 1:
-                ready = ready + list(prev[-1][0])
-            if step < n_units:
-                for g in gs:
-                    err_transpose(tiles, g)
-        for i in ready:
+            if 0 <= h - 2 < n_units:
+                nov_interleave(*units[h - 2])
+            if PRESORT <= h + LEAD < NT:
+                obs_sort(h + LEAD)
+            for vg, at, s_cols in ((0, VIL0, VIL0_S), (1, VIL1, VIL1_S)):
+                if h == at:
+                    v_interleave(vg, s_cols)
+                if h == at + 1:
+                    v_quantize(vg)
+            if 0 <= h - 1 < n_units:
+                err_transpose(*units[h - 1])
+        for i in range(next_bonus, NT):
             bonus(i)

from contextlib import ExitStack

import concourse.mybir as mybir
from concourse.masks import make_identity

M, K, F, D, R = 2048, 1024, 1024, 1024, 512
FLOPS = 2 * M * K * F + 2 * D * F * R + 2 * M * F * R

F32 = mybir.dt.float32
BF16 = mybir.dt.bfloat16
I32 = mybir.dt.int32
U32 = mybir.dt.uint32
U8 = mybir.dt.uint8
FP8X4 = mybir.dt.float8_e4m3fn_x4
FP4X4 = mybir.dt.float4_e2m1fn_x4
ALU = mybir.AluOpType
ACT = mybir.ActivationFunctionType

P = 128
PACK = 4
KP = P * PACK
NG = 2
NT = M // P
V_HEAD = 5
B_FIRST = 7
W10_V = 512
W01_V = 256
W11_V = 256
VIL0 = 1
VIL1 = 4
TAILV = 2
PRESORT = 8
VIL0_S = 256
VIL1_S = 256
B_LAST = 18
V_COPY = 4
W00_V = 256
T0 = 4
LEAD = 5
V2 = 1
SORT_S = 8
HEAD_SORT = 0
EARLYQ = 1
SINGLE = 1
RV0 = 10
RV1 = 16
RVP = 1


def tile_skill_novelty_bonus_s12_kernel(
    tc, obs, w, target, gain, code_words, code_scales, skill_words, skill_scales, out
):
    nc = tc.nc
    with ExitStack() as ctx:
        keep = ctx.enter_context(tc.tile_pool(name="keep", bufs=1))
        work = ctx.enter_context(tc.tile_pool(name="work", bufs=2))
        psum = ctx.enter_context(tc.psum_pool(name="psum", bufs=8))
        ctx.enter_context(tc.manual_schedule())

        def bank(name):
            return psum.tile([P, KP], F32, name=name, tag="bank")

        ident = keep.tile([P, P], F32, name="ident")
        make_identity(nc, ident[:])
        a_scale_raw = keep.tile([P, NG, F], U8, name="a_scale_raw", align_bytes=64)
        b_scale = keep.tile([P, NG, R], U8, name="b_scale", align_bytes=64)
        gain_rows32 = keep.tile([P, NG * P], F32, name="gain_rows32")
        half = keep.tile([P, NG * PACK], F32, name="half")
        nc.gpsimd.memset(half[:], 0.5)
        nc.vector.memset(a_scale_raw[:].rearrange("p g n -> p (g n)").bitcast(I32), 0)
        nc.vector.memset(b_scale[:].rearrange("p g n -> p (g n)").bitcast(I32), 0)
        nc.vector.memset(gain_rows32[:], 0.0)
        warm = keep.tile([P, 1], F32, name="warm")
        nc.scalar.activation(out=warm[:], in_=half[:, 0:1], func=ACT.Square)

        obs_sb, tgt_sb, w_raw = {}, {}, {}

        def load_obs(tiles):
            n = len(tiles)
            t = keep.tile([P, n, K], BF16, name="obs%d" % tiles[0], align_bytes=64)
            rows = obs[tiles[0] * P : (tiles[0] + n) * P, :]
            nc.sync.dma_start(out=t[:], in_=rows.rearrange("(i p) k -> p i k", p=P))
            for j, i in enumerate(tiles):
                obs_sb[i] = t[:, j, :]

        def load_target(tiles, gs):
            n = len(tiles)
            width = KP * len(gs)
            t = keep.tile([P, n, width], BF16, name="tgt%d_%d" % (tiles[0], gs[0]), align_bytes=64)
            rows = target[tiles[0] * P : (tiles[0] + n) * P, gs[0] * KP : gs[0] * KP + width]
            nc.sync.dma_start(out=t[:], in_=rows.rearrange("(i p) k -> p i k", p=P))
            for j, i in enumerate(tiles):
                for jg, g in enumerate(gs):
                    tgt_sb[i, g] = t[:, j, jg * KP : (jg + 1) * KP]

        def load_w(kg, g):
            t = keep.tile([P, PACK, KP], BF16, name="w%d%d" % (kg, g), align_bytes=64)
            rows = w[kg * KP : (kg + 1) * KP, g * KP : (g + 1) * KP]
            nc.sync.dma_start(out=t[:], in_=rows.rearrange("(p j) n -> p j n", j=PACK))
            w_raw[kg, g] = t

        gain_rows = keep.tile([PACK, NG * P], BF16, name="gain_rows")
        a_raw = keep.tile([P, NG, 2 * F], U8, name="a_raw", align_bytes=64)
        b_words = keep.tile([P, NG, 2 * R], U8, name="b_words", align_bytes=64)

        def load_scales(queue, plane, rows):
            for q in range(4):
                queue.dma_start(
                    out=plane[32 * q : 32 * q + 4, :, :].bitcast(I32),
                    in_=rows[:, 4 * q : 4 * q + 4, :].rearrange("g r n -> r g n").bitcast(I32),
                )

        units = [((0, 1), 0), ((2, 3), 0), ((0, 1), 1), ((2, 3), 1)]
        units += [((i, i + 1), g) for i in range(4, NT, 2) for g in range(NG)]
        units = units[:-SINGLE] + [((i,), g) for tiles, g in units[-SINGLE:] for i in tiles]

        nc.sync.dma_start(
            out=gain_rows[:].rearrange("t (q r) -> t q r", r=8),
            in_=gain.rearrange("(q t r) -> t q r", t=PACK, r=8),
        )
        load_scales(nc.sync, a_scale_raw, code_scales)
        load_obs((0, 1))
        nc.sync.dma_start(out=a_raw[:].bitcast(I32), in_=code_words.rearrange("g p n -> p g n").bitcast(I32))
        nc.sync.dma_start(out=b_words[:].bitcast(I32), in_=skill_words.rearrange("g p n -> p g n").bitcast(I32))
        load_scales(nc.sync, b_scale, skill_scales)
        load_w(0, 0)
        load_w(1, 0)
        load_obs((2, 3))
        load_target((0, 1), (0,))
        load_w(0, 1)
        load_target((2, 3), (0,))
        load_w(1, 1)
        load_obs((4, 5))
        load_target((0, 1, 2, 3), (1,))
        for i in range(6, NT, 2):
            load_obs((i, i + 1))
            load_target((i - 2, i - 1), (0, 1))
        load_target((NT - 2, NT - 1), (0, 1))

        def interleave(engine, dst, src):
            d = dst.rearrange("p (c i) t -> p c t i", i=4)
            s = src.rearrange("p t (c i) -> p c t i", i=4)
            if engine == "v":
                nc.vector.tensor_copy(out=d, in_=s)
            else:
                nc.scalar.copy(out=d, in_=s)

        def grouped_tile(name):
            return work.tile([P, KP, PACK], BF16, name=name, tag="grouped", bufs=4, align_bytes=64)

        def quantize(codes, scales, grouped):
            nc.vector.quantize_mx(out=codes.bitcast(FP8X4), scales=scales, in_=grouped)

        w_grouped, w_codes, w_scales = {}, {}, {}

        def w_interleave(kg, g, vec_cols):
            t = grouped_tile("wg%d%d" % (kg, g))
            if vec_cols:
                interleave("v", t[:, :vec_cols, :], w_raw[kg, g][:, :, :vec_cols])
            if vec_cols < KP:
                interleave("s", t[:, vec_cols:, :], w_raw[kg, g][:, :, vec_cols:])
            w_grouped[kg, g] = t

        def w_quantize(kg, g):
            w_codes[kg, g] = keep.tile([P, KP], U32, name="wc%d%d" % (kg, g), align_bytes=64)
            w_scales[kg, g] = keep.tile([P, KP], U8, name="ws%d%d" % (kg, g), align_bytes=64)
            quantize(w_codes[kg, g][:], w_scales[kg, g][:], w_grouped[kg, g][:].rearrange("p c t -> p (c t)"))

        obs_grouped, obs_codes, obs_scales = {}, {}, {}

        obs_sorted = {}

        def obs_sort(i):
            t = work.tile([P, NG, 2, P], F32, name="osort%d" % i, tag="osort", bufs=3, align_bytes=64)
            words = obs_sb[i].bitcast(F32)
            if i < SORT_S:
                nc.vector.tensor_copy(out=t[:], in_=words.rearrange("p (g j u) -> p g u j", g=NG, u=2))
            else:
                nc.scalar.copy(out=t[:], in_=words.rearrange("p (g j u) -> p g u j", g=NG, u=2))
            obs_sorted[i] = t

        def obs_transpose(i):
            words = obs_sb[i].bitcast(F32)
            b = bank("obsT%d" % i)
            for kg in range(NG):
                for u in range(2):
                    j = 2 * kg + u
                    if i in obs_sorted:
                        src = obs_sorted[i][:, kg, u, :]
                    else:
                        src = words[:, 256 * kg + u : 256 * (kg + 1) : 2]
                    nc.tensor.transpose(b[:, j * P : (j + 1) * P], src, ident[:])
            t = work.tile([P, NG, P, 2], F32, name="og%d" % i, tag="og", bufs=4, align_bytes=64)
            nc.scalar.copy(out=t[:], in_=b[:].rearrange("p (g u m) -> p g m u", g=NG, u=2))
            obs_grouped[i] = t

        def obs_quantize(i):
            obs_codes[i] = work.tile([P, NG * P], U32, name="oc%d" % i, tag="oc", bufs=8, align_bytes=64)
            obs_scales[i] = work.tile([P, NG * P], U8, name="os%d" % i, tag="os", bufs=8, align_bytes=64)
            quantize(
                obs_codes[i][:],
                obs_scales[i][:],
                obs_grouped[i][:].rearrange("p g m u -> p (g m u)").bitcast(BF16),
            )

        err = {}

        def predict(i, g):
            b = bank("pred%d_%d" % (i, g))
            for kg in range(NG):
                cols = slice(kg * P, (kg + 1) * P)
                nc.tensor.matmul_mx(
                    out=b[:],
                    lhsT=obs_codes[i][:, cols].bitcast(FP8X4),
                    lhsT_scale=obs_scales[i][:, cols],
                    rhs=w_codes[kg, g][:].bitcast(FP8X4),
                    rhs_scale=w_scales[kg, g][:],
                    start=(kg == 0),
                    stop=(kg == NG - 1),
                )
            e = work.tile([P, KP], F32, name="err%d_%d" % (i, g), tag="err", bufs=6, align_bytes=64)
            nc.vector.tensor_tensor(
                out=e[:].rearrange("p (t q r) -> p t q r", t=PACK, r=8),
                in0=b[:].rearrange("p (q t r) -> p t q r", t=PACK, r=8),
                in1=tgt_sb[i, g].rearrange("p (q t r) -> p t q r", t=PACK, r=8),
                op=ALU.subtract,
            )
            err[i, g] = e

        gain_root = keep.tile([P, NG * PACK], F32, name="gain_root")
        gain_sign = keep.tile([P, NG * PACK], F32, name="gain_sign")

        def gain_setup_transpose():
            nc.vector.tensor_copy(out=gain_rows32[0:PACK, :], in_=gain_rows[:])
            b = bank("gainT")
            for g in range(NG):
                nc.tensor.transpose(b[:, g * P : (g + 1) * P], gain_rows32[:, g * P : (g + 1) * P], ident[:])
            by_part = b[:, : NG * P].rearrange("p (g c) -> p g c", g=NG)[:, :, 0:PACK]
            twice = keep.tile([P, NG * PACK], F32, name="twice")
            mag = keep.tile([P, NG * PACK], F32, name="mag")
            nc.vector.tensor_scalar(twice[:].rearrange("p (g t) -> p g t", g=NG), by_part, 0.0, 2.0, ALU.is_ge, ALU.mult)
            nc.vector.tensor_scalar(gain_sign[:], twice[:], -1.0, None, ALU.add)
            nc.vector.tensor_tensor(
                out=mag[:].rearrange("p (g t) -> p g t", g=NG),
                in0=by_part,
                in1=gain_sign[:].rearrange("p (g t) -> p g t", g=NG),
                op=ALU.mult,
            )
            nc.gpsimd.tensor_tensor(out=gain_root[:], in0=mag[:], in1=half[:], op=ALU.pow)

        squares, nov_grouped, nov_codes, nov_scales = {}, {}, {}, {}

        def err_transpose(tiles, g):
            n = len(tiles)
            width = n * P
            sq = work.tile([P, PACK, width], BF16, name="sq%d_%d" % (tiles[0], g), tag="sq", bufs=4, align_bytes=64)
            per_bank = PACK // n
            for t0 in range(0, PACK, per_bank):
                b = bank("errT%d_%d_%d" % (tiles[0], g, t0))
                for s in range(per_bank):
                    for j, i in enumerate(tiles):
                        c0 = s * width + j * P
                        t = t0 + s
                        nc.tensor.transpose(b[:, c0 : c0 + P], err[i, g][:, t * P : (t + 1) * P], ident[:])
                for s in range(per_bank):
                    t = t0 + s
                    nc.scalar.activation(
                        out=sq[:, t, :],
                        in_=b[:, s * width : (s + 1) * width],
                        func=ACT.Square,
                        scale=gain_root[:, g * PACK + t : g * PACK + t + 1],
                    )
            squares[tiles, g] = sq

        def nov_interleave(tiles, g):
            t = grouped_tile("ng%d_%d" % (tiles[0], g))
            width = len(tiles) * P
            interleave("v", t[:, :width, :], squares[tiles, g][:])
            nov_grouped[tiles, g] = t

        def nov_quantize(tiles, g):
            width = len(tiles) * P
            c = work.tile([P, width], U32, name="nc%d_%d" % (tiles[0], g), tag="nc", bufs=12, align_bytes=64)
            s = work.tile([P, width], U8, name="ns%d_%d" % (tiles[0], g), tag="ns", bufs=12, align_bytes=64)
            quantize(c[:], s[:], nov_grouped[tiles, g][:, :width, :].rearrange("p c t -> p (c t)"))
            for j, i in enumerate(tiles):
                nov_codes[i, g] = c[:, j * P : (j + 1) * P]
                nov_scales[i, g] = s[:, j * P : (j + 1) * P]

        a_words = keep.tile([P, NG, 2 * F], U8, name="a_words", align_bytes=64)
        a_scale = keep.tile([P, NG, F], U8, name="a_scale", align_bytes=64)

        def a_permute():
            for dst, src, run in ((a_words, a_raw, 4), (a_scale, a_scale_raw, 2)):
                d = dst[:].rearrange("p g n -> p (g n)").bitcast(I32)
                s = src[:].rearrange("p g n -> p (g n)").bitcast(I32)
                nc.vector.tensor_copy(
                    out=d.rearrange("p (h t q r) -> p h t q r", t=PACK, q=16, r=run),
                    in_=s.rearrange("p (h q t r) -> p h t q r", t=PACK, q=16, r=run),
                )

        v_rows, v_grouped, v_codes, v_scales, v_banks = {}, {}, {}, {}, {}

        def v_matmul(g, t):
            if t == 0:
                v_rows[g] = work.tile([P, PACK, R], BF16, name="vr%d" % g, tag="vr", bufs=2, align_bytes=64)
            b = bank("v%d_%d" % (g, t))
            c0 = g * KP + t * P
            for dg in range(NG):
                nc.tensor.matmul_mx(
                    out=b[:],
                    lhsT=a_words[:, dg, 2 * c0 : 2 * (c0 + P)].bitcast(FP4X4),
                    lhsT_scale=a_scale[:, dg, c0 : c0 + P],
                    rhs=b_words[:, dg, :].bitcast(FP4X4),
                    rhs_scale=b_scale[:, dg, :],
                    start=(dg == 0),
                    stop=(dg == NG - 1),
                )
            v_banks[g, t] = b

        def v_copy(g, t):
            nc.scalar.activation(
                out=v_rows[g][:, t, :],
                in_=v_banks[g, t][:],
                func=ACT.Copy,
                scale=gain_sign[:, g * PACK + t : g * PACK + t + 1],
            )

        def v_interleave(g, s_cols):
            v_grouped[g] = grouped_tile("vg%d" % g)
            if s_cols < R:
                interleave("v", v_grouped[g][:, s_cols:, :], v_rows[g][:, :, s_cols:])
            if s_cols:
                interleave("s", v_grouped[g][:, :s_cols, :], v_rows[g][:, :, :s_cols])

        def v_quantize(g):
            v_codes[g] = keep.tile([P, R], U32, name="vc%d" % g, align_bytes=64)
            v_scales[g] = keep.tile([P, R], U8, name="vs%d" % g, align_bytes=64)
            quantize(v_codes[g][:], v_scales[g][:], v_grouped[g][:].rearrange("p c t -> p (c t)"))

        def bonus(i):
            b = bank("bonus%d" % i)
            for g in range(NG):
                nc.tensor.matmul_mx(
                    out=b[:],
                    lhsT=nov_codes[i, g].bitcast(FP8X4),
                    lhsT_scale=nov_scales[i, g],
                    rhs=v_codes[g][:].bitcast(FP8X4),
                    rhs_scale=v_scales[g][:],
                    start=(g == 0),
                    stop=(g == NG - 1),
                )
            res = work.tile([P, R], F32, name="res%d" % i, tag="res", bufs=6)
            if RV0 <= i < RV1 and i % 2 == RVP:
                nc.vector.tensor_copy(out=res[:], in_=b[:])
            else:
                nc.scalar.copy(out=res[:], in_=b[:])
            nc.sync.dma_start(out=out[i * P : (i + 1) * P, :], in_=res[:])

        v_jobs = [(g, t) for g in range(NG) for t in range(PACK)]
        gain_setup_transpose()
        obs_transpose(0)
        obs_transpose(1)
        a_permute()
        obs_quantize(0)
        obs_quantize(1)
        w_interleave(0, 0, W00_V)
        for g, t in v_jobs[:T0]:
            v_matmul(g, t)
            v_copy(g, t)
        w_quantize(0, 0)
        w_interleave(1, 0, W10_V)
        for g, t in v_jobs[T0:V_HEAD]:
            v_matmul(g, t)
        w_quantize(1, 0)
        for g, t in v_jobs[T0:V_COPY]:
            v_copy(g, t)
        if HEAD_SORT:
            obs_sort(2)
            obs_sort(3)
        obs_transpose(2)
        obs_transpose(3)
        for g, t in v_jobs[max(T0, V_COPY):V_HEAD]:
            v_copy(g, t)
        if EARLYQ:
            obs_quantize(2)
            obs_quantize(3)
        v_jobs = v_jobs[V_HEAD:]

        n_units = len(units)
        next_bonus = 0
        for h in range(n_units + 3):
            live = h < n_units
            if live:
                tiles, g = units[h]
                predict(tiles[0], g)
            if 0 <= h - 3 < n_units:
                nov_quantize(*units[h - 3])
            if h == 0 and not EARLYQ:
                obs_quantize(2)
            if h >= 2 and h + 2 < NT:
                obs_quantize(h + 2)
            if live and len(tiles) > 1:
                predict(tiles[1], g)
            if h == 0 and not EARLYQ:
                obs_quantize(3)
            if h == 0:
                w_interleave(0, 1, W01_V)
            if h == 1:
                w_quantize(0, 1)
                w_interleave(1, 1, W11_V)
            if v_jobs:
                n_v = 2 if h == V2 else 1
                for job in v_jobs[:n_v]:
                    v_matmul(*job)
                    v_copy(*job)
                v_jobs = v_jobs[n_v:]
            elif B_FIRST <= h <= B_LAST:
                bonus(next_bonus)
                next_bonus = next_bonus + 1
            if h >= 1 and h + 3 < NT:
                obs_transpose(h + 3)
            if h == 1:
                w_quantize(1, 1)
            if 0 <= h - 2 < n_units:
                nov_interleave(*units[h - 2])
            if PRESORT <= h + LEAD < NT:
                obs_sort(h + LEAD)
            for vg, at, s_cols in ((0, VIL0, VIL0_S), (1, VIL1, VIL1_S)):
                if h == at:
                    v_interleave(vg, s_cols)
                if h == at + 1:
                    v_quantize(vg)
            if 0 <= h - 1 < n_units:
                err_transpose(*units[h - 1])
        for i in range(next_bonus, NT):
            bonus(i)
